import numpy as np
import ml_dtypes


def mxq(x, axis, fmt="e4m3"):
    dtype, down = {"e4m3": (ml_dtypes.float8_e4m3fn, 7), "e5m2": (ml_dtypes.float8_e5m2, 14)}[fmt]
    v = np.moveaxis(np.asarray(x, np.float32).astype(ml_dtypes.bfloat16).astype(np.float64), axis, -1)
    blocks = v.reshape(v.shape[:-1] + (-1, 32))
    amax = np.abs(blocks).max(-1, keepdims=True)
    byte = np.maximum(np.where(amax > 0, np.frexp(amax)[1] - 1 + 127, 0) - down, 1)
    scale = np.exp2(byte - 127.0)
    codes = (blocks / scale).astype(np.float32).astype(dtype).astype(np.float64)
    return np.moveaxis((codes * scale).reshape(v.shape), -1, axis)


WIDE = False


def mx_kscale(k):
    if not WIDE:
        return np.ones(k)
    levels = np.array([10, -10, 5, -5, 0])
    if k % 512:
        return np.exp2(np.random.permutation(np.resize(levels, k // 32))).repeat(32)
    a = np.empty((k // 512, 16))
    for p in range(k // 512):
        a[p, :8] = np.random.permutation(np.resize(levels, 8))
        for g in range(8):
            far = levels[np.abs(levels - a[p, g]) >= 10]
            a[p, g + 8] = far[np.random.randint(len(far))]
    return np.exp2(a.ravel()).repeat(32)


def f64(x):
    return np.asarray(x).astype(np.float64)


def striped(idx):
    return np.tile(idx.reshape(-1, 16).T, (8, 1)).astype(np.uint16)


def unstriped(offs):
    return offs[:16].T.reshape(-1).astype(np.int64)


def striped8(idx):
    return np.concatenate([x.reshape(-1, 16).T for x in idx]).astype(np.uint16)


def runs(offs, k):
    lists = np.stack([offs[16 * r : 16 * r + 16].T.reshape(-1) for r in range(8)]).astype(np.int64)
    return lists[np.arange(k) % 512 // 64]


def pack_weight(w):
    k, n = w.shape
    w = f64(np.asarray(w, np.float32).astype(ml_dtypes.bfloat16)).reshape(k // 32, 32, n)
    amax = np.abs(w).max(1)
    byte = np.clip(np.where(amax > 0, np.frexp(amax)[1] - 1 + 127 - 7, 1), 1, 254)
    scaled = (w * np.exp2(127.0 - byte)[:, None, :]).reshape(k, n).astype(np.float32)
    words = np.ascontiguousarray(scaled.reshape(k // 512, 128, 4, n).transpose(0, 1, 3, 2)).astype(ml_dtypes.float8_e4m3fn).view(np.uint8)
    return words, np.ascontiguousarray(byte.astype(np.uint8).reshape(k // 512, 16, n))


def unpack_weight(words, scales):
    g, p, n, _ = words.shape
    vals = np.ascontiguousarray(words).view(ml_dtypes.float8_e4m3fn).astype(np.float64) * np.repeat(np.exp2(scales.astype(np.float64) - 127.0), 8, axis=1)[..., None]
    return vals.transpose(0, 1, 3, 2).reshape(g * 512, n)


K, T, S, N, H = 512, 2048, 512, 512, 512


def setup_inputs():
    n = np.random.standard_normal
    s = mx_kscale(K)[:, None]
    u = mx_kscale(H)
    packed_xT = pack_weight(n((K, T)) * s)
    return {
        "x_words": packed_xT[0],
        "x_scales": packed_xT[1],
        "w1": (n((K, H)) / np.sqrt(K) / s).astype(np.float32),
        "gn": (np.random.uniform(0.5, 1.5, (H, 1)) * u[:, None]).astype(np.float32),
        "w2": (n((H, N)) / np.sqrt(H) / u[:, None]).astype(np.float32),
        "res": (2 * n((N, S))).astype(np.float32),
        "offs": striped(np.random.permutation(T)[:S]),
        "rt": striped8(np.stack([np.random.permutation(S) for _ in range(8)])),
        "lf": striped8(np.stack([np.random.permutation(S) for _ in range(8)])),
    }


def reference(x_words, x_scales, w1, gn, w2, res, offs, rt, lf):
    xq = unpack_weight(x_words, x_scales)[:, unstriped(offs)]
    y = mxq(f64(w1), 0, "e4m3").T @ xq
    d = y[np.arange(H)[:, None], runs(rt, H)] - y
    p = d / (np.sqrt((d) ** 2 + 1))
    z = f64(gn) * (p - (p[np.arange(H)[:, None], runs(lf, H)]))
    return f64(res) + (mxq(f64(w2), 0, "e4m3").T @ mxq(z, 0, "e4m3"))

@@ -1,0 +1,182 @@
+from contextlib import ExitStack
+
+import concourse.mybir as mybir
+
+K, T, S, H, N = 512, 2048, 512, 512, 512
+FLOPS = 2 * K * H * S + 2 * H * N * S
+
+F32 = mybir.dt.float32
+BF16 = mybir.dt.bfloat16
+I32 = mybir.dt.int32
+U32 = mybir.dt.uint32
+U16 = mybir.dt.uint16
+U8 = mybir.dt.uint8
+FP8X4 = mybir.dt.float8_e4m3fn_x4
+ACT = mybir.ActivationFunctionType
+ALU = mybir.AluOpType
+
+P = 128
+PACK = 4
+QUADRANT = 32
+BANK = 512
+HALF = S // 2
+LIST_ROWS = 16
+CHUNKS = ((0, 256), (256, 384), (384, 512))
+W1_SCALAR_COLS = 96
+
+
+def tile_picked_curvflow_none_p_kernel(
+    tc, x_words, x_scales, w1, gn, w2, res, offs, rt, lf, out
+):
+    nc = tc.nc
+    with ExitStack() as ctx:
+        lists = ctx.enter_context(tc.tile_pool(name="lists", bufs=1))
+        sb = ctx.enter_context(tc.tile_pool(name="sb", bufs=1))
+        ps = ctx.enter_context(tc.psum_pool(name="ps", bufs=1))
+
+        offs_sb = lists.tile([P, S // LIST_ROWS], U16, name="offs_sb")
+        rt_sb = lists.tile([P, S // LIST_ROWS], U16, name="rt_sb")
+        lf_sb = lists.tile([P, S // LIST_ROWS], U16, name="lf_sb")
+
+        def entries(list_sb, lo, hi):
+            return list_sb[:, lo // LIST_ROWS : hi // LIST_ROWS]
+
+        def gather(on_scalar, dst, window, offsets):
+            if on_scalar:
+                nc.scalar.activation(out=dst, in_=window.indirect(offsets), func=ACT.Copy)
+            else:
+                nc.vector.tensor_copy(out=dst, in_=window.indirect(offsets))
+
+        def copy(on_scalar, dst, src):
+            if on_scalar:
+                nc.scalar.copy(out=dst, in_=src)
+            else:
+                nc.vector.tensor_copy(out=dst, in_=src)
+
+        xs_rows = sb.tile([P, T // PACK], I32, name="xs_rows")
+        for q in range(4):
+            nc.scalar.dma_start(
+                out=xs_rows[QUADRANT * q : QUADRANT * q + 4, :],
+                in_=x_scales[0, 4 * q : 4 * q + 4, :].bitcast(I32),
+            )
+        w1_raw = sb.tile([P, PACK, H], F32, name="w1_raw")
+        nc.sync.dma_start(out=w1_raw[:], in_=w1.rearrange("(p j) c -> p j c", j=PACK))
+        nc.sync.dma_start(out=offs_sb[:], in_=offs)
+        xw_all = sb.tile([P, T], I32, name="xw_all", align_bytes=64)
+        nc.sync.dma_start(out=xw_all[:], in_=x_words[0].rearrange("p c r -> p (c r)").bitcast(I32))
+        nc.sync.dma_start(out=rt_sb[:], in_=rt)
+        w2_raw = sb.tile([P, PACK, N], F32, name="w2_raw")
+        nc.sync.dma_start(out=w2_raw[:], in_=w2.rearrange("(p j) c -> p j c", j=PACK))
+        gn_sb = sb.tile([P, PACK], F32, name="gn_sb")
+        nc.sync.dma_start(out=gn_sb[:], in_=gn.rearrange("(p t) o -> p (t o)", t=PACK))
+        nc.sync.dma_start(out=lf_sb[:], in_=lf)
+        res_sb = sb.tile([P, N // P, S], F32, name="res_sb")
+        nc.sync.dma_start(out=res_sb[:], in_=res.rearrange("(b p) c -> p b c", p=P))
+
+        xs_all = sb.tile([P, T], U8, name="xs_all", align_bytes=64)
+        nc.vector.memset(xs_all[:].bitcast(I32), 0)
+        for q in range(4):
+            rows = slice(QUADRANT * q, QUADRANT * q + 4)
+            nc.vector.tensor_copy(out=xs_all[rows, :].bitcast(I32), in_=xs_rows[rows, :])
+        xs = sb.tile([P, S], U8, name="xs", align_bytes=64)
+        nc.vector.tensor_copy(out=xs[:], in_=xs_all[:].indirect(offs_sb[:]))
+
+        w1_bf = sb.tile([P, PACK, P, PACK], BF16, name="w1_bf", align_bytes=64)
+        for on_scalar, lo, hi in ((True, 0, W1_SCALAR_COLS), (False, W1_SCALAR_COLS, P)):
+            copy(
+                on_scalar,
+                w1_bf[:, :, lo:hi, :].rearrange("p t m j -> p m t j"),
+                w1_raw[:, :, PACK * lo : PACK * hi].rearrange("p j (m t) -> p m t j", t=PACK),
+            )
+        w1_codes = sb.tile([P, H], U32, name="w1_codes", align_bytes=64)
+        w1_scales = sb.tile([P, H], U8, name="w1_scales", align_bytes=64)
+        nc.vector.quantize_mx(
+            out=w1_codes[:].bitcast(FP8X4), scales=w1_scales[:], in_=w1_bf[:].rearrange("p t m j -> p (t m j)")
+        )
+
+        xw = [sb.tile([P, HALF], U32, name=f"xw{h}", align_bytes=64) for h in range(2)]
+        y_ps = [ps.tile([P, S], F32, name=f"y_ps{t}") for t in range(PACK)]
+        for h in range(2):
+            offsets = entries(offs_sb, h * HALF, (h + 1) * HALF)
+            nc.vector.tensor_copy(out=xw[h][:], in_=xw_all[:].bitcast(U32).indirect(offsets))
+        for t in range(PACK):
+            for h in range(2):
+                nc.tensor.matmul_mx(
+                    out=y_ps[t][:, h * HALF : (h + 1) * HALF],
+                    lhsT=w1_codes[:, t * P : (t + 1) * P].bitcast(FP8X4),
+                    lhsT_scale=w1_scales[:, t * P : (t + 1) * P],
+                    rhs=xw[h][:].bitcast(FP8X4),
+                    rhs_scale=xs[:, h * HALF : (h + 1) * HALF],
+                    start=True,
+                    stop=True,
+                )
+
+        w2_bf = sb.tile([P, N, PACK], BF16, name="w2_bf", align_bytes=64)
+        w2_codes = sb.tile([P, N], U32, name="w2_codes", align_bytes=64)
+        w2_scales = sb.tile([P, N], U8, name="w2_scales", align_bytes=64)
+        for lo in (0, N // 2):
+            nc.gpsimd.tensor_scalar(
+                out=w2_bf[:, lo : lo + N // 2, :],
+                in0=w2_raw[:, :, lo : lo + N // 2].rearrange("p j c -> p c j"),
+                scalar1=1.0,
+                scalar2=0.0,
+                op0=ALU.mult,
+                op1=ALU.add,
+            )
+
+        gp = []
+        for t in range(PACK):
+            y = sb.tile([P, S], F32, name=f"y{t}")
+            copy(t % 2 == 0, y[:], y_ps[t][:])
+            y_right = sb.tile([P, S], F32, name=f"y_right{t}")
+            for h in range(2):
+                lo, hi = h * HALF, (h + 1) * HALF
+                gather(h == 0 or t == PACK - 1, y_right[:, lo:hi], y[:], entries(rt_sb, lo, hi))
+            d = sb.tile([P, S], F32, name=f"d{t}")
+            nc.vector.tensor_tensor(out=d[:], in0=y_right[:], in1=y_ps[t][:], op=ALU.subtract)
+            d_sq = sb.tile([P, S], F32, name=f"d_sq{t}")
+            nc.scalar.activation(out=d_sq[:], in_=d[:], func=ACT.Square)
+            inv_norm = sb.tile([P, S], F32, name=f"inv_norm{t}")
+            nc.scalar.activation(out=inv_norm[:], in_=d_sq[:], func=ACT.Abs_reciprocal_sqrt, bias=1.0)
+            gp_t = sb.tile([P, S], F32, name=f"gp{t}")
+            nc.vector.scalar_tensor_tensor(
+                out=gp_t[:], in0=d[:], scalar=gn_sb[:, t : t + 1], in1=inv_norm[:], op0=ALU.mult, op1=ALU.mult
+            )
+            gp.append(gp_t)
+
+        nc.vector.quantize_mx(
+            out=w2_codes[:].bitcast(FP8X4), scales=w2_scales[:], in_=w2_bf[:].rearrange("p c j -> p (c j)")
+        )
+
+        out_rows = out.rearrange("(b p) c -> p b c", p=P)
+        for c, (lo, hi) in enumerate(CHUNKS):
+            width = hi - lo
+            z = sb.tile([P, PACK, width], BF16, name=f"z{c}")
+            for t in range(PACK):
+                gp_left = sb.tile([P, width], F32, name=f"gp_left{c}_{t}")
+                gather(t != 0, gp_left[:], gp[t][:], entries(lf_sb, lo, hi))
+                nc.vector.tensor_tensor(out=z[:, t, :], in0=gp[t][:, lo:hi], in1=gp_left[:], op=ALU.subtract)
+            z_bf = sb.tile([P, width, PACK], BF16, name=f"z_bf{c}", align_bytes=64)
+            copy(c % 2 == 0, z_bf[:], z[:].rearrange("p t c -> p c t"))
+            z_codes = sb.tile([P, width], U32, name=f"z_codes{c}", align_bytes=64)
+            z_scales = sb.tile([P, width], U8, name=f"z_scales{c}", align_bytes=64)
+            nc.vector.quantize_mx(
+                out=z_codes[:].bitcast(FP8X4), scales=z_scales[:], in_=z_bf[:].rearrange("p c t -> p (c t)")
+            )
+            per_bank = BANK // width
+            for b0 in range(0, N // P, per_bank):
+                acc = ps.tile([P, per_bank, width], F32, name=f"acc{c}_{b0}")
+                for e in range(per_bank):
+                    b = b0 + e
+                    nc.tensor.matmul_mx(
+                        out=acc[:, e, :],
+                        lhsT=w2_codes[:, b * P : (b + 1) * P].bitcast(FP8X4),
+                        lhsT_scale=w2_scales[:, b * P : (b + 1) * P],
+                        rhs=z_codes[:].bitcast(FP8X4),
+                        rhs_scale=z_scales[:],
+                        start=True,
+                        stop=True,
+                    )
+                o = sb.tile([P, per_bank, width], F32, name=f"o{c}_{b0}")
+                nc.vector.tensor_tensor(out=o[:], in0=acc[:], in1=res_sb[:, b0 : b0 + per_bank, lo:hi], op=ALU.add)
+                nc.sync.dma_start(out=out_rows[:, b0 : b0 + per_bank, lo:hi], in_=o[:])

@@ -22,7 +22,7 @@ BANK = 512
 HALF = S // 2
 LIST_ROWS = 16
 CHUNKS = ((0, 256), (256, 384), (384, 512))
-W1_SCALAR_COLS = 96
+W1_SCALAR_COLS = 80
 
 
 def tile_picked_curvflow_none_p_kernel(
@@ -55,7 +55,7 @@ def tile_picked_curvflow_none_p_kernel(
 
         xs_rows = sb.tile([P, T // PACK], I32, name="xs_rows")
         for q in range(4):
-            nc.scalar.dma_start(
+            nc.sync.dma_start(
                 out=xs_rows[QUADRANT * q : QUADRANT * q + 4, :],
                 in_=x_scales[0, 4 * q : 4 * q + 4, :].bitcast(I32),
             )
@@ -72,6 +72,11 @@ def tile_picked_curvflow_none_p_kernel(
         nc.sync.dma_start(out=lf_sb[:], in_=lf)
         res_sb = sb.tile([P, N // P, S], F32, name="res_sb")
         nc.sync.dma_start(out=res_sb[:], in_=res.rearrange("(b p) c -> p b c", p=P))
+
+        warm_in = sb.tile([P, 1], F32, name="warm_in")
+        warm_out = sb.tile([P, 1], F32, name="warm_out")
+        nc.gpsimd.memset(warm_in[:], 1.0)
+        nc.scalar.activation(out=warm_out[:], in_=warm_in[:], func=ACT.Abs_reciprocal_sqrt, bias=1.0)
 
         xs_all = sb.tile([P, T], U8, name="xs_all", align_bytes=64)
         nc.vector.memset(xs_all[:].bitcast(I32), 0)

@@ -53,6 +53,13 @@ def tile_picked_curvflow_none_p_kernel(
             else:
                 nc.vector.tensor_copy(out=dst, in_=src)
 
+        def interleave(on_scalar, dst, src):
+            copy(
+                on_scalar,
+                dst.rearrange("p (c i) t -> p c t i", i=PACK),
+                src.rearrange("p t (c i) -> p c t i", i=PACK),
+            )
+
         xs_rows = sb.tile([P, T // PACK], I32, name="xs_rows")
         for q in range(4):
             nc.sync.dma_start(
@@ -65,8 +72,10 @@ def tile_picked_curvflow_none_p_kernel(
         xw_all = sb.tile([P, T], I32, name="xw_all", align_bytes=64)
         nc.sync.dma_start(out=xw_all[:], in_=x_words[0].rearrange("p c r -> p (c r)").bitcast(I32))
         nc.sync.dma_start(out=rt_sb[:], in_=rt)
-        w2_raw = sb.tile([P, PACK, N], F32, name="w2_raw")
-        nc.sync.dma_start(out=w2_raw[:], in_=w2.rearrange("(p j) c -> p j c", j=PACK))
+        w2_raw = [sb.tile([P, PACK, N // 2], F32, name=f"w2_raw{h}") for h in range(2)]
+        w2_rows = w2.rearrange("(p j) c -> p j c", j=PACK)
+        for h in range(2):
+            nc.sync.dma_start(out=w2_raw[h][:], in_=w2_rows[:, :, h * (N // 2) : (h + 1) * (N // 2)])
         gn_sb = sb.tile([P, PACK], F32, name="gn_sb")
         nc.sync.dma_start(out=gn_sb[:], in_=gn.rearrange("(p t) o -> p (t o)", t=PACK))
         nc.sync.dma_start(out=lf_sb[:], in_=lf)
@@ -90,8 +99,8 @@ def tile_picked_curvflow_none_p_kernel(
         for on_scalar, lo, hi in ((True, 0, W1_SCALAR_COLS), (False, W1_SCALAR_COLS, P)):
             copy(
                 on_scalar,
-                w1_bf[:, :, lo:hi, :].rearrange("p t m j -> p m t j"),
-                w1_raw[:, :, PACK * lo : PACK * hi].rearrange("p j (m t) -> p m t j", t=PACK),
+                w1_bf[:, :, lo:hi, :].rearrange("p t m j -> p m j t"),
+                w1_raw[:, :, PACK * lo : PACK * hi].rearrange("p j (m t) -> p m j t", t=PACK),
             )
         w1_codes = sb.tile([P, H], U32, name="w1_codes", align_bytes=64)
         w1_scales = sb.tile([P, H], U8, name="w1_scales", align_bytes=64)
@@ -119,10 +128,10 @@ def tile_picked_curvflow_none_p_kernel(
         w2_bf = sb.tile([P, N, PACK], BF16, name="w2_bf", align_bytes=64)
         w2_codes = sb.tile([P, N], U32, name="w2_codes", align_bytes=64)
         w2_scales = sb.tile([P, N], U8, name="w2_scales", align_bytes=64)
-        for lo in (0, N // 2):
+        for h in range(2):
             nc.gpsimd.tensor_scalar(
-                out=w2_bf[:, lo : lo + N // 2, :],
-                in0=w2_raw[:, :, lo : lo + N // 2].rearrange("p j c -> p c j"),
+                out=w2_bf[:, h * (N // 2) : (h + 1) * (N // 2), :],
+                in0=w2_raw[h][:].rearrange("p j c -> p c j"),
                 scalar1=1.0,
                 scalar2=0.0,
                 op0=ALU.mult,
@@ -132,11 +141,11 @@ def tile_picked_curvflow_none_p_kernel(
         gp = []
         for t in range(PACK):
             y = sb.tile([P, S], F32, name=f"y{t}")
-            copy(t % 2 == 0, y[:], y_ps[t][:])
+            copy(t == 0, y[:], y_ps[t][:])
             y_right = sb.tile([P, S], F32, name=f"y_right{t}")
             for h in range(2):
                 lo, hi = h * HALF, (h + 1) * HALF
-                gather(h == 0 or t == PACK - 1, y_right[:, lo:hi], y[:], entries(rt_sb, lo, hi))
+                gather(h == 0 or t < 2, y_right[:, lo:hi], y[:], entries(rt_sb, lo, hi))
             d = sb.tile([P, S], F32, name=f"d{t}")
             nc.vector.tensor_tensor(out=d[:], in0=y_right[:], in1=y_ps[t][:], op=ALU.subtract)
             d_sq = sb.tile([P, S], F32, name=f"d_sq{t}")
@@ -159,10 +168,10 @@ def tile_picked_curvflow_none_p_kernel(
             z = sb.tile([P, PACK, width], BF16, name=f"z{c}")
             for t in range(PACK):
                 gp_left = sb.tile([P, width], F32, name=f"gp_left{c}_{t}")
-                gather(t != 0, gp_left[:], gp[t][:], entries(lf_sb, lo, hi))
+                gather(c > 0 or t == PACK - 1, gp_left[:], gp[t][:], entries(lf_sb, lo, hi))
                 nc.vector.tensor_tensor(out=z[:, t, :], in0=gp[t][:, lo:hi], in1=gp_left[:], op=ALU.subtract)
             z_bf = sb.tile([P, width, PACK], BF16, name=f"z_bf{c}", align_bytes=64)
-            copy(c % 2 == 0, z_bf[:], z[:].rearrange("p t c -> p c t"))
+            interleave(c % 2 == 0, z_bf[:], z[:])
             z_codes = sb.tile([P, width], U32, name=f"z_codes{c}", align_bytes=64)
             z_scales = sb.tile([P, width], U8, name=f"z_scales{c}", align_bytes=64)
             nc.vector.quantize_mx(
@@ -182,6 +191,12 @@ def tile_picked_curvflow_none_p_kernel(
                         start=True,
                         stop=True,
                     )
-                o = sb.tile([P, per_bank, width], F32, name=f"o{c}_{b0}")
-                nc.vector.tensor_tensor(out=o[:], in0=acc[:], in1=res_sb[:, b0 : b0 + per_bank, lo:hi], op=ALU.add)
-                nc.sync.dma_start(out=out_rows[:, b0 : b0 + per_bank, lo:hi], in_=o[:])
+                pieces = 2 if c == len(CHUNKS) - 1 else 1
+                n = per_bank // pieces
+                for e0 in range(0, per_bank, n):
+                    blocks = slice(b0 + e0, b0 + e0 + n)
+                    o = sb.tile([P, n, width], F32, name=f"o{c}_{b0 + e0}")
+                    nc.vector.tensor_tensor(
+                        out=o[:], in0=acc[:, e0 : e0 + n, :], in1=res_sb[:, blocks, lo:hi], op=ALU.add
+                    )
+                    nc.sync.dma_start(out=out_rows[:, blocks, lo:hi], in_=o[:])

from contextlib import ExitStack

import concourse.mybir as mybir

K, T, S, H, N = 512, 2048, 512, 512, 512
FLOPS = 2 * K * H * S + 2 * H * N * S

F32 = mybir.dt.float32
BF16 = mybir.dt.bfloat16
I32 = mybir.dt.int32
U32 = mybir.dt.uint32
U16 = mybir.dt.uint16
U8 = mybir.dt.uint8
FP8X4 = mybir.dt.float8_e4m3fn_x4
ACT = mybir.ActivationFunctionType
ALU = mybir.AluOpType

P = 128
PACK = 4
QUADRANT = 32
BANK = 512
HALF = S // 2
LIST_ROWS = 16
CHUNKS = ((0, 256), (256, 384), (384, 512))
W1_SCALAR_COLS = 80


def tile_picked_curvflow_none_p_kernel(
    tc, x_words, x_scales, w1, gn, w2, res, offs, rt, lf, out
):
    nc = tc.nc
    with ExitStack() as ctx:
        lists = ctx.enter_context(tc.tile_pool(name="lists", bufs=1))
        sb = ctx.enter_context(tc.tile_pool(name="sb", bufs=1))
        ps = ctx.enter_context(tc.psum_pool(name="ps", bufs=1))

        offs_sb = lists.tile([P, S // LIST_ROWS], U16, name="offs_sb")
        rt_sb = lists.tile([P, S // LIST_ROWS], U16, name="rt_sb")
        lf_sb = lists.tile([P, S // LIST_ROWS], U16, name="lf_sb")

        def entries(list_sb, lo, hi):
            return list_sb[:, lo // LIST_ROWS : hi // LIST_ROWS]

        def gather(on_scalar, dst, window, offsets):
            if on_scalar:
                nc.scalar.activation(out=dst, in_=window.indirect(offsets), func=ACT.Copy)
            else:
                nc.vector.tensor_copy(out=dst, in_=window.indirect(offsets))

        def copy(on_scalar, dst, src):
            if on_scalar:
                nc.scalar.copy(out=dst, in_=src)
            else:
                nc.vector.tensor_copy(out=dst, in_=src)

        def interleave(on_scalar, dst, src):
            copy(
                on_scalar,
                dst.rearrange("p (c i) t -> p c t i", i=PACK),
                src.rearrange("p t (c i) -> p c t i", i=PACK),
            )

        xs_rows = sb.tile([P, T // PACK], I32, name="xs_rows")
        for q in range(4):
            nc.sync.dma_start(
                out=xs_rows[QUADRANT * q : QUADRANT * q + 4, :],
                in_=x_scales[0, 4 * q : 4 * q + 4, :].bitcast(I32),
            )
        w1_raw = sb.tile([P, PACK, H], F32, name="w1_raw")
        nc.sync.dma_start(out=w1_raw[:], in_=w1.rearrange("(p j) c -> p j c", j=PACK))
        nc.sync.dma_start(out=offs_sb[:], in_=offs)
        xw_all = sb.tile([P, T], I32, name="xw_all", align_bytes=64)
        nc.sync.dma_start(out=xw_all[:], in_=x_words[0].rearrange("p c r -> p (c r)").bitcast(I32))
        nc.sync.dma_start(out=rt_sb[:], in_=rt)
        w2_raw = [sb.tile([P, PACK, N // 2], F32, name=f"w2_raw{h}") for h in range(2)]
        w2_rows = w2.rearrange("(p j) c -> p j c", j=PACK)
        for h in range(2):
            nc.sync.dma_start(out=w2_raw[h][:], in_=w2_rows[:, :, h * (N // 2) : (h + 1) * (N // 2)])
        gn_sb = sb.tile([P, PACK], F32, name="gn_sb")
        nc.sync.dma_start(out=gn_sb[:], in_=gn.rearrange("(p t) o -> p (t o)", t=PACK))
        nc.sync.dma_start(out=lf_sb[:], in_=lf)
        res_sb = sb.tile([P, N // P, S], F32, name="res_sb")
        nc.sync.dma_start(out=res_sb[:], in_=res.rearrange("(b p) c -> p b c", p=P))

        warm_in = sb.tile([P, 1], F32, name="warm_in")
        warm_out = sb.tile([P, 1], F32, name="warm_out")
        nc.gpsimd.memset(warm_in[:], 1.0)
        nc.scalar.activation(out=warm_out[:], in_=warm_in[:], func=ACT.Abs_reciprocal_sqrt, bias=1.0)

        xs_all = sb.tile([P, T], U8, name="xs_all", align_bytes=64)
        nc.vector.memset(xs_all[:].bitcast(I32), 0)
        for q in range(4):
            rows = slice(QUADRANT * q, QUADRANT * q + 4)
            nc.vector.tensor_copy(out=xs_all[rows, :].bitcast(I32), in_=xs_rows[rows, :])
        xs = sb.tile([P, S], U8, name="xs", align_bytes=64)
        nc.vector.tensor_copy(out=xs[:], in_=xs_all[:].indirect(offs_sb[:]))

        w1_bf = sb.tile([P, PACK, P, PACK], BF16, name="w1_bf", align_bytes=64)
        for on_scalar, lo, hi in ((True, 0, W1_SCALAR_COLS), (False, W1_SCALAR_COLS, P)):
            copy(
                on_scalar,
                w1_bf[:, :, lo:hi, :].rearrange("p t m j -> p m j t"),
                w1_raw[:, :, PACK * lo : PACK * hi].rearrange("p j (m t) -> p m j t", t=PACK),
            )
        w1_codes = sb.tile([P, H], U32, name="w1_codes", align_bytes=64)
        w1_scales = sb.tile([P, H], U8, name="w1_scales", align_bytes=64)
        nc.vector.quantize_mx(
            out=w1_codes[:].bitcast(FP8X4), scales=w1_scales[:], in_=w1_bf[:].rearrange("p t m j -> p (t m j)")
        )

        xw = [sb.tile([P, HALF], U32, name=f"xw{h}", align_bytes=64) for h in range(2)]
        y_ps = [ps.tile([P, S], F32, name=f"y_ps{t}") for t in range(PACK)]
        for h in range(2):
            offsets = entries(offs_sb, h * HALF, (h + 1) * HALF)
            nc.vector.tensor_copy(out=xw[h][:], in_=xw_all[:].bitcast(U32).indirect(offsets))
        for t in range(PACK):
            for h in range(2):
                nc.tensor.matmul_mx(
                    out=y_ps[t][:, h * HALF : (h + 1) * HALF],
                    lhsT=w1_codes[:, t * P : (t + 1) * P].bitcast(FP8X4),
                    lhsT_scale=w1_scales[:, t * P : (t + 1) * P],
                    rhs=xw[h][:].bitcast(FP8X4),
                    rhs_scale=xs[:, h * HALF : (h + 1) * HALF],
                    start=True,
                    stop=True,
                )

        w2_bf = sb.tile([P, N, PACK], BF16, name="w2_bf", align_bytes=64)
        w2_codes = sb.tile([P, N], U32, name="w2_codes", align_bytes=64)
        w2_scales = sb.tile([P, N], U8, name="w2_scales", align_bytes=64)
        for h in range(2):
            nc.gpsimd.tensor_scalar(
                out=w2_bf[:, h * (N // 2) : (h + 1) * (N // 2), :],
                in0=w2_raw[h][:].rearrange("p j c -> p c j"),
                scalar1=1.0,
                scalar2=0.0,
                op0=ALU.mult,
                op1=ALU.add,
            )

        gp = []
        for t in range(PACK):
            y = sb.tile([P, S], F32, name=f"y{t}")
            copy(t == 0, y[:], y_ps[t][:])
            y_right = sb.tile([P, S], F32, name=f"y_right{t}")
            for h in range(2):
                lo, hi = h * HALF, (h + 1) * HALF
                gather(h == 0 or t < 2, y_right[:, lo:hi], y[:], entries(rt_sb, lo, hi))
            d = sb.tile([P, S], F32, name=f"d{t}")
            nc.vector.tensor_tensor(out=d[:], in0=y_right[:], in1=y_ps[t][:], op=ALU.subtract)
            d_sq = sb.tile([P, S], F32, name=f"d_sq{t}")
            nc.scalar.activation(out=d_sq[:], in_=d[:], func=ACT.Square)
            inv_norm = sb.tile([P, S], F32, name=f"inv_norm{t}")
            nc.scalar.activation(out=inv_norm[:], in_=d_sq[:], func=ACT.Abs_reciprocal_sqrt, bias=1.0)
            gp_t = sb.tile([P, S], F32, name=f"gp{t}")
            nc.vector.scalar_tensor_tensor(
                out=gp_t[:], in0=d[:], scalar=gn_sb[:, t : t + 1], in1=inv_norm[:], op0=ALU.mult, op1=ALU.mult
            )
            gp.append(gp_t)

        nc.vector.quantize_mx(
            out=w2_codes[:].bitcast(FP8X4), scales=w2_scales[:], in_=w2_bf[:].rearrange("p c j -> p (c j)")
        )

        out_rows = out.rearrange("(b p) c -> p b c", p=P)
        for c, (lo, hi) in enumerate(CHUNKS):
            width = hi - lo
            z = sb.tile([P, PACK, width], BF16, name=f"z{c}")
            for t in range(PACK):
                gp_left = sb.tile([P, width], F32, name=f"gp_left{c}_{t}")
                gather(c > 0 or t == PACK - 1, gp_left[:], gp[t][:], entries(lf_sb, lo, hi))
                nc.vector.tensor_tensor(out=z[:, t, :], in0=gp[t][:, lo:hi], in1=gp_left[:], op=ALU.subtract)
            z_bf = sb.tile([P, width, PACK], BF16, name=f"z_bf{c}", align_bytes=64)
            interleave(c % 2 == 0, z_bf[:], z[:])
            z_codes = sb.tile([P, width], U32, name=f"z_codes{c}", align_bytes=64)
            z_scales = sb.tile([P, width], U8, name=f"z_scales{c}", align_bytes=64)
            nc.vector.quantize_mx(
                out=z_codes[:].bitcast(FP8X4), scales=z_scales[:], in_=z_bf[:].rearrange("p c t -> p (c t)")
            )
            per_bank = BANK // width
            for b0 in range(0, N // P, per_bank):
                acc = ps.tile([P, per_bank, width], F32, name=f"acc{c}_{b0}")
                for e in range(per_bank):
                    b = b0 + e
                    nc.tensor.matmul_mx(
                        out=acc[:, e, :],
                        lhsT=w2_codes[:, b * P : (b + 1) * P].bitcast(FP8X4),
                        lhsT_scale=w2_scales[:, b * P : (b + 1) * P],
                        rhs=z_codes[:].bitcast(FP8X4),
                        rhs_scale=z_scales[:],
                        start=True,
                        stop=True,
                    )
                pieces = 2 if c == len(CHUNKS) - 1 else 1
                n = per_bank // pieces
                for e0 in range(0, per_bank, n):
                    blocks = slice(b0 + e0, b0 + e0 + n)
                    o = sb.tile([P, n, width], F32, name=f"o{c}_{b0 + e0}")
                    nc.vector.tensor_tensor(
                        out=o[:], in0=acc[:, e0 : e0 + n, :], in1=res_sb[:, blocks, lo:hi], op=ALU.add
                    )
                    nc.sync.dma_start(out=out_rows[:, blocks, lo:hi], in_=o[:])
